import numpy as np
import ml_dtypes


def mxq(x, axis, fmt="e4m3"):
    dtype, down = {"e4m3": (ml_dtypes.float8_e4m3fn, 7), "e5m2": (ml_dtypes.float8_e5m2, 14)}[fmt]
    v = np.moveaxis(np.asarray(x, np.float32).astype(ml_dtypes.bfloat16).astype(np.float64), axis, -1)
    blocks = v.reshape(v.shape[:-1] + (-1, 32))
    amax = np.abs(blocks).max(-1, keepdims=True)
    byte = np.maximum(np.where(amax > 0, np.frexp(amax)[1] - 1 + 127, 0) - down, 1)
    scale = np.exp2(byte - 127.0)
    codes = (blocks / scale).astype(np.float32).astype(dtype).astype(np.float64)
    return np.moveaxis((codes * scale).reshape(v.shape), -1, axis)


WIDE = False


def mx_kscale(k):
    if not WIDE:
        return np.ones(k)
    levels = np.array([10, -10, 5, -5, 0])
    if k % 512:
        return np.exp2(np.random.permutation(np.resize(levels, k // 32))).repeat(32)
    a = np.empty((k // 512, 16))
    for p in range(k // 512):
        a[p, :8] = np.random.permutation(np.resize(levels, 8))
        for g in range(8):
            far = levels[np.abs(levels - a[p, g]) >= 10]
            a[p, g + 8] = far[np.random.randint(len(far))]
    return np.exp2(a.ravel()).repeat(32)


def f64(x):
    return np.asarray(x).astype(np.float64)


def striped(idx):
    return np.tile(idx.reshape(-1, 16).T, (8, 1)).astype(np.uint16)


def unstriped(offs):
    return offs[:16].T.reshape(-1).astype(np.int64)


def striped8(idx):
    return np.concatenate([x.reshape(-1, 16).T for x in idx]).astype(np.uint16)


def runs(offs, k):
    lists = np.stack([offs[16 * r : 16 * r + 16].T.reshape(-1) for r in range(8)]).astype(np.int64)
    return lists[np.arange(k) % 512 // 64]


def pack_weight(w):
    k, n = w.shape
    w = f64(np.asarray(w, np.float32).astype(ml_dtypes.bfloat16)).reshape(k // 32, 32, n)
    amax = np.abs(w).max(1)
    byte = np.clip(np.where(amax > 0, np.frexp(amax)[1] - 1 + 127 - 7, 1), 1, 254)
    scaled = (w * np.exp2(127.0 - byte)[:, None, :]).reshape(k, n).astype(np.float32)
    words = np.ascontiguousarray(scaled.reshape(k // 512, 128, 4, n).transpose(0, 1, 3, 2)).astype(ml_dtypes.float8_e4m3fn).view(np.uint8)
    return words, np.ascontiguousarray(byte.astype(np.uint8).reshape(k // 512, 16, n))


def unpack_weight(words, scales):
    g, p, n, _ = words.shape
    vals = np.ascontiguousarray(words).view(ml_dtypes.float8_e4m3fn).astype(np.float64) * np.repeat(np.exp2(scales.astype(np.float64) - 127.0), 8, axis=1)[..., None]
    return vals.transpose(0, 1, 3, 2).reshape(g * 512, n)


K, T, S, H, W = 512, 2048, 512, 512, 256


def setup_inputs():
    n = np.random.standard_normal
    s = mx_kscale(K)[:, None]
    u = mx_kscale(S)
    packed_xT = pack_weight(n((K, T)) * s)
    perm = np.stack([np.random.permutation(S) for _ in range(8)])
    return {
        "x_words": packed_xT[0],
        "x_scales": packed_xT[1],
        "w1": (n((K, H)) / np.sqrt(K) / s).astype(np.float32),
        "ga": (np.random.uniform(0.5, 1.5, (H, 1)) * u[:, None]).astype(np.float32),
        "gb": (np.random.uniform(0.5, 1.5, (H, 1)) / u[:, None]).astype(np.float32),
        "offs": striped(np.random.permutation(T)[:S]),
        "n1": striped8(perm[:, :W]),
        "n2": striped8(perm[:, W:]),
        "n3": striped8(np.stack([np.random.permutation(S) for _ in range(8)])),
        "n4": striped8(np.stack([np.random.permutation(S) for _ in range(8)])),
        "n5": striped8(np.stack([np.random.permutation(S) for _ in range(8)])),
        "n6": striped8(np.stack([np.random.permutation(S) for _ in range(8)])),
    }


def reference(x_words, x_scales, w1, ga, gb, offs, n1, n2, n3, n4, n5, n6):
    xq = unpack_weight(x_words, x_scales)[:, unstriped(offs)]
    y = mxq(f64(w1), 0, "e4m3").T @ xq
    pa = y[np.arange(H)[:, None], runs(n1, H)]
    pb = y[np.arange(H)[:, None], runs(n2, H)]
    rb = np.maximum(pa, pb)
    ra = pa / (np.abs(pb) + 0.5)
    ds = np.zeros((H, S))
    ds[np.arange(H)[:, None], runs(n1, H)] = ra
    dt = ds.copy()
    dt[np.arange(H)[:, None], runs(n2, H)] = rb
    z = f64(ga) * dt
    ex = np.exp(0.5 * y)
    z2 = f64(gb) * ((2.0 * ex) / (ex + ex[np.arange(H)[:, None], runs(n3, H)] + ex[np.arange(H)[:, None], runs(n4, H)]))
    s = 0.0625 * ((mxq(z, 0, "e4m3").T @ mxq(z2, 0, "e4m3")))
    return s * (s[np.arange(S)[:, None], runs(n5, S)] - (s[np.arange(S)[:, None], runs(n6, S)]))

@@ -1,0 +1,179 @@
+import concourse.mybir as mybir
+from concourse.masks import make_identity
+
+K, T, S, H, W = 512, 2048, 512, 512, 256
+FLOPS = 2 * K * H * S + 2 * H * S * S
+
+F32 = mybir.dt.float32
+BF16 = mybir.dt.bfloat16
+I32 = mybir.dt.int32
+U32 = mybir.dt.uint32
+U16 = mybir.dt.uint16
+U8 = mybir.dt.uint8
+FP8X4 = mybir.dt.float8_e4m3fn_x4
+ALU = mybir.AluOpType
+ACT = mybir.ActivationFunctionType
+
+P = 128
+PACK = 4
+HALF = S // 2
+
+
+def tile_picked_selfratiosharewind_none_p_kernel(
+    tc, x_words, x_scales, w1, ga, gb, offs, n1, n2, n3, n4, n5, n6, out
+):
+    nc = tc.nc
+    tiles = range(PACK)
+    with (
+        tc.tile_pool(name="lists", bufs=1) as lists,
+        tc.tile_pool(name="keep", bufs=1) as keep,
+        tc.psum_pool(name="psum", bufs=1) as psum,
+    ):
+        banks = [psum.tile([P, S], F32, name=f"bank{b}") for b in range(8)]
+
+        def load_list(name, src):
+            tile = lists.tile(list(src.shape), U16, name=name)
+            nc.sync.dma_start(tile[:], src)
+            return tile
+
+        xs = keep.tile([P, T], U8, name="xs")
+        nc.vector.memset(xs[:].bitcast(I32), 0)
+        offs_sb = load_list("offs_sb", offs)
+        w_raw = keep.tile([P, PACK, H], F32, name="w_raw")
+        nc.sync.dma_start(w_raw[:], w1.rearrange("(p j) c -> p j c", j=PACK))
+        for q in range(4):
+            nc.sync.dma_start(xs[32 * q : 32 * q + 4, :].bitcast(I32), x_scales[0, 4 * q : 4 * q + 4, :].bitcast(I32))
+        xw = keep.tile([P, T], I32, name="xw")
+        nc.sync.dma_start(xw[:], x_words[0].rearrange("p n t -> p (n t)").bitcast(I32))
+        n2_sb = load_list("n2_sb", n2)
+        n1_sb = load_list("n1_sb", n1)
+        n3_sb = load_list("n3_sb", n3)
+        n4_sb = load_list("n4_sb", n4)
+        n6_sb = load_list("n6_sb", n6)
+        n5_sb = load_list("n5_sb", n5)
+
+        ident = keep.tile([P, P], F32, name="ident")
+        make_identity(nc, ident[:])
+        ga_sb = keep.tile([P, PACK], F32, name="ga_sb")
+        gb_sb = keep.tile([P, PACK], F32, name="gb_sb")
+        nc.gpsimd.dma_start(ga_sb[:], ga.rearrange("(p t) o -> p (t o)", t=PACK))
+        nc.gpsimd.dma_start(gb_sb[:], gb.rearrange("(p t) o -> p (t o)", t=PACK))
+
+        rows = [keep.tile([P, 2 * S], F32, name=f"rows{t}") for t in tiles]
+        for t in tiles:
+            nc.vector.memset(rows[t][:, S:], 0.0)
+        warm = keep.tile([P, 1], F32, name="warm")
+        nc.scalar.activation(warm[:], rows[0][:, S : S + 1], ACT.Abs_reciprocal_sqrt, bias=0.5)
+
+        xsg = keep.tile([P, S], U8, name="xsg", align_bytes=64)
+        nc.vector.tensor_copy(xsg[:], xs[:].indirect(offs_sb[:]))
+        wi = keep.tile([P, PACK, P, PACK], BF16, name="wi", align_bytes=64)
+        nc.vector.tensor_copy(wi[:].rearrange("p t m j -> p m j t"), w_raw[:].rearrange("p j (m t) -> p m j t", t=PACK))
+        wq = keep.tile([P, H], U32, name="wq", align_bytes=64)
+        ws = keep.tile([P, H], U8, name="ws", align_bytes=64)
+        nc.vector.quantize_mx(wq[:].bitcast(FP8X4), ws[:], wi[:].rearrange("p t m j -> p (t m j)"))
+        xg = keep.tile([P, S], U32, name="xg", align_bytes=64)
+        nc.vector.tensor_copy(xg[:], xw[:].bitcast(U32).indirect(offs_sb[:]))
+
+        for t in tiles:
+            cols = slice(P * t, P * (t + 1))
+            nc.tensor.matmul_mx(
+                banks[t][:], lhsT=wq[:, cols].bitcast(FP8X4), lhsT_scale=ws[:, cols],
+                rhs=xg[:].bitcast(FP8X4), rhs_scale=xsg[:], start=True, stop=True,
+            )
+        for t in tiles:
+            nc.scalar.copy(rows[t][:, :S], banks[t][:])
+
+        pa = keep.tile([P, PACK, W], F32, name="pa")
+        pb = keep.tile([P, PACK, W], F32, name="pb")
+        rb = keep.tile([P, PACK, W], F32, name="rb")
+        inv = keep.tile([P, PACK, W], F32, name="inv")
+        exps = [keep.tile([P, 3, S], F32, name=f"exps{t}") for t in tiles]
+        for t in tiles:
+            nc.vector.tensor_copy(pb[:, t, :], rows[t][:].indirect(n2_sb[:]))
+        for t in tiles:
+            nc.vector.tensor_copy(pa[:, t, :], rows[t][:].indirect(n1_sb[:]))
+        for t in tiles:
+            size = exps[t][:, 0:2, 0 : W // 2]
+            root = exps[t][:, 2, 0:W]
+            nc.scalar.activation(size, pb[:, t, :].rearrange("p (a b) -> p a b", a=2), ACT.Abs)
+            nc.scalar.activation(root.rearrange("p (a b) -> p a b", a=2), size, ACT.Abs_reciprocal_sqrt, bias=0.5)
+            nc.scalar.activation(inv[:, t, :], root, ACT.Square)
+        for u in range(2):
+            pair = slice(2 * u, 2 * u + 2)
+            nc.vector.tensor_tensor(rb[:, pair, :], pa[:, pair, :], pb[:, pair, :], ALU.max)
+        dt = [keep.tile([P, S], F32, name=f"dt{t}") for t in tiles]
+        for t in tiles:
+            nc.vector.tensor_copy(dt[t][:].indirect(n2_sb[:]), rb[:, t, :])
+        for t in tiles:
+            nc.vector.tensor_tensor(dt[t][:].indirect(n1_sb[:]), pa[:, t, :], inv[:, t, :], ALU.mult)
+
+        for t in tiles:
+            nc.scalar.activation(exps[t][:, 0, :], banks[t][:], ACT.Exp, scale=0.5)
+            nc.scalar.activation(exps[t][:, 1, :], rows[t][:].indirect(n3_sb[:]), ACT.Exp, scale=0.5)
+            nc.scalar.activation(exps[t][:, 2, :], rows[t][:].indirect(n4_sb[:]), ACT.Exp, scale=0.5)
+            for b in range(4):
+                cols = slice(P * b, P * (b + 1))
+                for e in range(3):
+                    nc.tensor.matmul(
+                        banks[4 + t][:, cols], lhsT=exps[t][:, e, cols], rhs=ident[:],
+                        start=(e == 0), stop=(e == 2), is_transpose=True,
+                    )
+
+        zz = keep.tile([P, PACK, S], BF16, name="zz")
+        for t in tiles:
+            nc.vector.tensor_scalar(
+                zz[:, t, :].rearrange("p (u m) -> p m u", u=PACK), dt[t][:].rearrange("p (m u) -> p m u", u=PACK),
+                ga_sb[:, t : t + 1], None, ALU.mult,
+            )
+        zi = keep.tile([P, S, PACK], BF16, name="zi", align_bytes=64)
+        nc.vector.tensor_copy(zi[:], zz[:].rearrange("p t c -> p c t"))
+        zq = keep.tile([P, S], U32, name="zq", align_bytes=64)
+        zs = keep.tile([P, S], U8, name="zs", align_bytes=64)
+        nc.vector.quantize_mx(zq[:].bitcast(FP8X4), zs[:], zi[:].rearrange("p c t -> p (c t)"))
+
+        turned = [keep.tile([P, S], F32, name=f"turned{t}") for t in tiles]
+        for t in tiles:
+            nc.scalar.activation(turned[t][:], banks[4 + t][:], ACT.Abs_reciprocal_sqrt, scale=0.5)
+        share = keep.tile([P, PACK, S], F32, name="share")
+        for b in range(4):
+            cols = slice(P * b, P * (b + 1))
+            for t in tiles:
+                nc.tensor.transpose(banks[b][:, P * t : P * (t + 1)], turned[t][:, cols], ident[:])
+            nc.scalar.activation(share[:, :, cols], banks[b][:].rearrange("p (t c) -> p t c", t=PACK), ACT.Square)
+
+        z2z = keep.tile([P, PACK, S], BF16, name="z2z")
+        z2i = keep.tile([P, S, PACK], BF16, name="z2i", align_bytes=64)
+        z2q = keep.tile([P, S], U32, name="z2q", align_bytes=64)
+        z2s = keep.tile([P, S], U8, name="z2s", align_bytes=64)
+        for h in range(2):
+            half = slice(HALF * h, HALF * (h + 1))
+            for t in tiles:
+                nc.vector.scalar_tensor_tensor(
+                    z2z[:, t, half], share[:, t, half], gb_sb[:, t : t + 1], exps[t][:, 0, half], ALU.mult, ALU.mult
+                )
+            nc.vector.tensor_copy(z2i[:, half, :], z2z[:, :, half].rearrange("p t c -> p c t"))
+            nc.vector.quantize_mx(z2q[:, half].bitcast(FP8X4), z2s[:, half], z2i[:, half, :].rearrange("p c t -> p (c t)"))
+            for u in tiles:
+                cols = slice(P * u, P * (u + 1))
+                nc.tensor.matmul_mx(
+                    banks[4 + u][:, half], lhsT=zq[:, cols].bitcast(FP8X4), lhsT_scale=zs[:, cols],
+                    rhs=z2q[:, half].bitcast(FP8X4), rhs_scale=z2s[:, half], start=True, stop=True,
+                )
+        for u in tiles:
+            nc.scalar.activation(rows[u][:, :S], banks[4 + u][:], ACT.Copy, scale=0.0625)
+
+        second = [keep.tile([P, S], F32, name=f"second{u}") for u in tiles]
+        diff = [keep.tile([P, S], F32, name=f"diff{u}") for u in tiles]
+        result = [keep.tile([P, S], F32, name=f"result{u}") for u in tiles]
+        out_rows = out.rearrange("(p u) c -> u p c", u=PACK)
+        for step in range(PACK + 2):
+            if step < PACK:
+                nc.vector.tensor_copy(second[step][:], rows[step][:].indirect(n6_sb[:]))
+            if 1 <= step <= PACK:
+                u = step - 1
+                nc.vector.tensor_tensor(diff[u][:], rows[u][:].indirect(n5_sb[:]), second[u][:], ALU.subtract)
+            if step >= 2:
+                u = step - 2
+                nc.vector.tensor_tensor(result[u][:], diff[u][:], rows[u][:, :S], ALU.mult)
+                nc.sync.dma_start(out_rows[u], result[u][:])

@@ -16,7 +16,8 @@ ACT = mybir.ActivationFunctionType
 
 P = 128
 PACK = 4
-HALF = S // 2
+W_SPLIT = 64
+LAST = PACK - 1
 
 
 def tile_picked_selfratiosharewind_none_p_kernel(
@@ -36,13 +37,12 @@ def tile_picked_selfratiosharewind_none_p_kernel(
             nc.sync.dma_start(tile[:], src)
             return tile
 
-        xs = keep.tile([P, T], U8, name="xs")
-        nc.vector.memset(xs[:].bitcast(I32), 0)
         offs_sb = load_list("offs_sb", offs)
+        xs_in = keep.tile([P, T], U8, name="xs_in")
+        for q in range(4):
+            nc.sync.dma_start(xs_in[32 * q : 32 * q + 4, :].bitcast(I32), x_scales[0, 4 * q : 4 * q + 4, :].bitcast(I32))
         w_raw = keep.tile([P, PACK, H], F32, name="w_raw")
         nc.sync.dma_start(w_raw[:], w1.rearrange("(p j) c -> p j c", j=PACK))
-        for q in range(4):
-            nc.sync.dma_start(xs[32 * q : 32 * q + 4, :].bitcast(I32), x_scales[0, 4 * q : 4 * q + 4, :].bitcast(I32))
         xw = keep.tile([P, T], I32, name="xw")
         nc.sync.dma_start(xw[:], x_words[0].rearrange("p n t -> p (n t)").bitcast(I32))
         n2_sb = load_list("n2_sb", n2)
@@ -65,10 +65,17 @@ def tile_picked_selfratiosharewind_none_p_kernel(
         warm = keep.tile([P, 1], F32, name="warm")
         nc.scalar.activation(warm[:], rows[0][:, S : S + 1], ACT.Abs_reciprocal_sqrt, bias=0.5)
 
+        xs = keep.tile([P, T], U8, name="xs")
+        nc.vector.memset(xs[:].bitcast(I32), 0)
+        for q in range(4):
+            nc.vector.tensor_copy(xs[32 * q : 32 * q + 4, :].bitcast(I32), xs_in[32 * q : 32 * q + 4, :].bitcast(I32))
         xsg = keep.tile([P, S], U8, name="xsg", align_bytes=64)
         nc.vector.tensor_copy(xsg[:], xs[:].indirect(offs_sb[:]))
         wi = keep.tile([P, PACK, P, PACK], BF16, name="wi", align_bytes=64)
-        nc.vector.tensor_copy(wi[:].rearrange("p t m j -> p m j t"), w_raw[:].rearrange("p j (m t) -> p m j t", t=PACK))
+        wi_view = wi[:].rearrange("p t m j -> p m t j")
+        w_view = w_raw[:].rearrange("p j (m t) -> p m t j", t=PACK)
+        nc.vector.tensor_copy(wi_view[:, :W_SPLIT], w_view[:, :W_SPLIT])
+        nc.scalar.copy(wi_view[:, W_SPLIT:], w_view[:, W_SPLIT:])
         wq = keep.tile([P, H], U32, name="wq", align_bytes=64)
         ws = keep.tile([P, H], U8, name="ws", align_bytes=64)
         nc.vector.quantize_mx(wq[:].bitcast(FP8X4), ws[:], wi[:].rearrange("p t m j -> p (t m j)"))
@@ -81,7 +88,8 @@ def tile_picked_selfratiosharewind_none_p_kernel(
                 banks[t][:], lhsT=wq[:, cols].bitcast(FP8X4), lhsT_scale=ws[:, cols],
                 rhs=xg[:].bitcast(FP8X4), rhs_scale=xsg[:], start=True, stop=True,
             )
-        for t in tiles:
+        nc.vector.tensor_copy(rows[0][:, :S], banks[0][:])
+        for t in range(1, PACK):
             nc.scalar.copy(rows[t][:, :S], banks[t][:])
 
         pa = keep.tile([P, PACK, W], F32, name="pa")
@@ -104,9 +112,9 @@ def tile_picked_selfratiosharewind_none_p_kernel(
             nc.vector.tensor_tensor(rb[:, pair, :], pa[:, pair, :], pb[:, pair, :], ALU.max)
         dt = [keep.tile([P, S], F32, name=f"dt{t}") for t in tiles]
         for t in tiles:
-            nc.vector.tensor_copy(dt[t][:].indirect(n2_sb[:]), rb[:, t, :])
-        for t in tiles:
             nc.vector.tensor_tensor(dt[t][:].indirect(n1_sb[:]), pa[:, t, :], inv[:, t, :], ALU.mult)
+        for t in tiles:
+            nc.vector.tensor_copy(dt[t][:].indirect(n2_sb[:]), rb[:, t, :])
 
         for t in tiles:
             nc.scalar.activation(exps[t][:, 0, :], banks[t][:], ACT.Exp, scale=0.5)
@@ -116,52 +124,62 @@ def tile_picked_selfratiosharewind_none_p_kernel(
                 cols = slice(P * b, P * (b + 1))
                 for e in range(3):
                     nc.tensor.matmul(
-                        banks[4 + t][:, cols], lhsT=exps[t][:, e, cols], rhs=ident[:],
+                        banks[4 + b][:, P * t : P * (t + 1)], lhsT=exps[t][:, e, cols], rhs=ident[:],
                         start=(e == 0), stop=(e == 2), is_transpose=True,
                     )
 
         zz = keep.tile([P, PACK, S], BF16, name="zz")
-        for t in tiles:
-            nc.vector.tensor_scalar(
-                zz[:, t, :].rearrange("p (u m) -> p m u", u=PACK), dt[t][:].rearrange("p (m u) -> p m u", u=PACK),
-                ga_sb[:, t : t + 1], None, ALU.mult,
-            )
+        for t in range(LAST):
+            nc.gpsimd.tensor_scalar(zz[:, t, :], dt[t][:], ga_sb[:, t : t + 1], 0.0, ALU.mult, ALU.add)
+        nc.vector.tensor_scalar(zz[:, LAST, :], dt[LAST][:], ga_sb[:, LAST : LAST + 1], None, ALU.mult)
         zi = keep.tile([P, S, PACK], BF16, name="zi", align_bytes=64)
-        nc.vector.tensor_copy(zi[:], zz[:].rearrange("p t c -> p c t"))
+        nc.vector.tensor_copy(
+            zi[:].rearrange("p (u m) t -> p m u t", u=PACK), zz[:].rearrange("p t (m u) -> p m u t", u=PACK)
+        )
         zq = keep.tile([P, S], U32, name="zq", align_bytes=64)
         zs = keep.tile([P, S], U8, name="zs", align_bytes=64)
         nc.vector.quantize_mx(zq[:].bitcast(FP8X4), zs[:], zi[:].rearrange("p c t -> p (c t)"))
 
-        turned = [keep.tile([P, S], F32, name=f"turned{t}") for t in tiles]
-        for t in tiles:
-            nc.scalar.activation(turned[t][:], banks[4 + t][:], ACT.Abs_reciprocal_sqrt, scale=0.5)
+        turned = [keep.tile([P, H], F32, name=f"turned{b}") for b in range(4)]
         share = keep.tile([P, PACK, S], F32, name="share")
-        for b in range(4):
-            cols = slice(P * b, P * (b + 1))
-            for t in tiles:
-                nc.tensor.transpose(banks[b][:, P * t : P * (t + 1)], turned[t][:, cols], ident[:])
-            nc.scalar.activation(share[:, :, cols], banks[b][:].rearrange("p (t c) -> p t c", t=PACK), ACT.Square)
+        for step in range(5):
+            if step < 4:
+                b = step
+                nc.scalar.activation(turned[b][:], banks[4 + b][:], ACT.Abs_reciprocal_sqrt, scale=0.5)
+                for t in tiles:
+                    feats = slice(P * t, P * (t + 1))
+                    nc.tensor.transpose(banks[b][:, feats], turned[b][:, feats], ident[:])
+            if step >= 1:
+                b = step - 1
+                nc.scalar.activation(
+                    share[:, :, P * b : P * (b + 1)], banks[b][:].rearrange("p (t c) -> p t c", t=PACK), ACT.Square
+                )
 
         z2z = keep.tile([P, PACK, S], BF16, name="z2z")
         z2i = keep.tile([P, S, PACK], BF16, name="z2i", align_bytes=64)
         z2q = keep.tile([P, S], U32, name="z2q", align_bytes=64)
         z2s = keep.tile([P, S], U8, name="z2s", align_bytes=64)
-        for h in range(2):
-            half = slice(HALF * h, HALF * (h + 1))
+        for b in range(4):
+            places = slice(P * b, P * (b + 1))
             for t in tiles:
                 nc.vector.scalar_tensor_tensor(
-                    z2z[:, t, half], share[:, t, half], gb_sb[:, t : t + 1], exps[t][:, 0, half], ALU.mult, ALU.mult
+                    z2z[:, t, places], share[:, t, places], gb_sb[:, t : t + 1], exps[t][:, 0, places], ALU.mult, ALU.mult
                 )
-            nc.vector.tensor_copy(z2i[:, half, :], z2z[:, :, half].rearrange("p t c -> p c t"))
-            nc.vector.quantize_mx(z2q[:, half].bitcast(FP8X4), z2s[:, half], z2i[:, half, :].rearrange("p c t -> p (c t)"))
+            nc.vector.tensor_copy(z2i[:, places, :], z2z[:, :, places].rearrange("p t c -> p c t"))
+            nc.vector.quantize_mx(
+                z2q[:, places].bitcast(FP8X4), z2s[:, places], z2i[:, places, :].rearrange("p c t -> p (c t)")
+            )
+            if b == LAST:
+                for u in tiles:
+                    nc.scalar.activation(rows[u][:, : P * LAST], banks[4 + u][:, : P * LAST], ACT.Copy, scale=0.0625)
             for u in tiles:
                 cols = slice(P * u, P * (u + 1))
                 nc.tensor.matmul_mx(
-                    banks[4 + u][:, half], lhsT=zq[:, cols].bitcast(FP8X4), lhsT_scale=zs[:, cols],
-                    rhs=z2q[:, half].bitcast(FP8X4), rhs_scale=z2s[:, half], start=True, stop=True,
+                    banks[4 + u][:, places], lhsT=zq[:, cols].bitcast(FP8X4), lhsT_scale=zs[:, cols],
+                    rhs=z2q[:, places].bitcast(FP8X4), rhs_scale=z2s[:, places], start=True, stop=True,
                 )
         for u in tiles:
-            nc.scalar.activation(rows[u][:, :S], banks[4 + u][:], ACT.Copy, scale=0.0625)
+            nc.scalar.activation(rows[u][:, P * LAST : S], banks[4 + u][:, P * LAST :], ACT.Copy, scale=0.0625)
 
         second = [keep.tile([P, S], F32, name=f"second{u}") for u in tiles]
         diff = [keep.tile([P, S], F32, name=f"diff{u}") for u in tiles]
@@ -175,5 +193,6 @@ def tile_picked_selfratiosharewind_none_p_kernel(
                 nc.vector.tensor_tensor(diff[u][:], rows[u][:].indirect(n5_sb[:]), second[u][:], ALU.subtract)
             if step >= 2:
                 u = step - 2
-                nc.vector.tensor_tensor(result[u][:], diff[u][:], rows[u][:, :S], ALU.mult)
+                engine = nc.gpsimd if u < 2 else nc.vector
+                engine.tensor_tensor(result[u][:], diff[u][:], rows[u][:, :S], ALU.mult)
                 nc.sync.dma_start(out_rows[u], result[u][:])

@@ -16,7 +16,9 @@ ACT = mybir.ActivationFunctionType
 
 P = 128
 PACK = 4
-W_SPLIT = 64
+HALF = S // 2
+SCALAR_N4 = 3
+SUMMED = (1, 2)
 LAST = PACK - 1
 
 
@@ -40,7 +42,8 @@ def tile_picked_selfratiosharewind_none_p_kernel(
         offs_sb = load_list("offs_sb", offs)
         xs_in = keep.tile([P, T], U8, name="xs_in")
         for q in range(4):
-            nc.sync.dma_start(xs_in[32 * q : 32 * q + 4, :].bitcast(I32), x_scales[0, 4 * q : 4 * q + 4, :].bitcast(I32))
+            queue = nc.sync if q < 2 else nc.scalar
+            queue.dma_start(xs_in[32 * q : 32 * q + 4, :].bitcast(I32), x_scales[0, 4 * q : 4 * q + 4, :].bitcast(I32))
         w_raw = keep.tile([P, PACK, H], F32, name="w_raw")
         nc.sync.dma_start(w_raw[:], w1.rearrange("(p j) c -> p j c", j=PACK))
         xw = keep.tile([P, T], I32, name="xw")
@@ -56,14 +59,12 @@ def tile_picked_selfratiosharewind_none_p_kernel(
         make_identity(nc, ident[:])
         ga_sb = keep.tile([P, PACK], F32, name="ga_sb")
         gb_sb = keep.tile([P, PACK], F32, name="gb_sb")
-        nc.gpsimd.dma_start(ga_sb[:], ga.rearrange("(p t) o -> p (t o)", t=PACK))
-        nc.gpsimd.dma_start(gb_sb[:], gb.rearrange("(p t) o -> p (t o)", t=PACK))
+        nc.sync.dma_start(ga_sb[:], ga.rearrange("(p t) o -> p (t o)", t=PACK))
+        nc.sync.dma_start(gb_sb[:], gb.rearrange("(p t) o -> p (t o)", t=PACK))
 
         rows = [keep.tile([P, 2 * S], F32, name=f"rows{t}") for t in tiles]
         for t in tiles:
-            nc.vector.memset(rows[t][:, S:], 0.0)
-        warm = keep.tile([P, 1], F32, name="warm")
-        nc.scalar.activation(warm[:], rows[0][:, S : S + 1], ACT.Abs_reciprocal_sqrt, bias=0.5)
+            nc.gpsimd.memset(rows[t][:, S:], 0.0)
 
         xs = keep.tile([P, T], U8, name="xs")
         nc.vector.memset(xs[:].bitcast(I32), 0)
@@ -71,128 +72,188 @@ def tile_picked_selfratiosharewind_none_p_kernel(
             nc.vector.tensor_copy(xs[32 * q : 32 * q + 4, :].bitcast(I32), xs_in[32 * q : 32 * q + 4, :].bitcast(I32))
         xsg = keep.tile([P, S], U8, name="xsg", align_bytes=64)
         nc.vector.tensor_copy(xsg[:], xs[:].indirect(offs_sb[:]))
-        wi = keep.tile([P, PACK, P, PACK], BF16, name="wi", align_bytes=64)
-        wi_view = wi[:].rearrange("p t m j -> p m t j")
-        w_view = w_raw[:].rearrange("p j (m t) -> p m t j", t=PACK)
-        nc.vector.tensor_copy(wi_view[:, :W_SPLIT], w_view[:, :W_SPLIT])
-        nc.scalar.copy(wi_view[:, W_SPLIT:], w_view[:, W_SPLIT:])
         wq = keep.tile([P, H], U32, name="wq", align_bytes=64)
         ws = keep.tile([P, H], U8, name="ws", align_bytes=64)
-        nc.vector.quantize_mx(wq[:].bitcast(FP8X4), ws[:], wi[:].rearrange("p t m j -> p (t m j)"))
+        w_view = w_raw[:].rearrange("p j (m t) -> p m t j", t=PACK)
+        for g, copy in enumerate((nc.vector.tensor_copy, nc.scalar.copy)):
+            wi = keep.tile([P, 2, P, PACK], BF16, name=f"wi{g}", align_bytes=64)
+            copy(wi[:].rearrange("p t m j -> p m t j"), w_view[:, :, 2 * g : 2 * g + 2, :])
+            cols = slice(2 * P * g, 2 * P * (g + 1))
+            nc.vector.quantize_mx(wq[:, cols].bitcast(FP8X4), ws[:, cols], wi[:].rearrange("p t m j -> p (t m j)"))
         xg = keep.tile([P, S], U32, name="xg", align_bytes=64)
-        nc.vector.tensor_copy(xg[:], xw[:].bitcast(U32).indirect(offs_sb[:]))
+        for h in range(2):
+            entries = offs_sb[:, HALF // 16 * h : HALF // 16 * (h + 1)]
+            nc.vector.tensor_copy(xg[:, HALF * h : HALF * (h + 1)], xw[:].bitcast(U32).indirect(entries))
 
-        for t in tiles:
+
+        def project(t, places, bank):
             cols = slice(P * t, P * (t + 1))
             nc.tensor.matmul_mx(
-                banks[t][:], lhsT=wq[:, cols].bitcast(FP8X4), lhsT_scale=ws[:, cols],
-                rhs=xg[:].bitcast(FP8X4), rhs_scale=xsg[:], start=True, stop=True,
+                bank[:, places], lhsT=wq[:, cols].bitcast(FP8X4), lhsT_scale=ws[:, cols],
+                rhs=xg[:, places].bitcast(FP8X4), rhs_scale=xsg[:, places], start=True, stop=True,
             )
-        nc.vector.tensor_copy(rows[0][:, :S], banks[0][:])
+
+        project(0, slice(0, HALF), banks[4])
+        nc.scalar.copy(rows[0][:, :HALF], banks[4][:, :HALF])
+        project(0, slice(HALF, S), banks[0])
+        nc.vector.tensor_copy(rows[0][:, HALF:S], banks[0][:, HALF:])
         for t in range(1, PACK):
+            project(t, slice(0, S), banks[t])
+        nc.vector.tensor_copy(rows[1][:, :S], banks[1][:])
+        for t in range(2, PACK):
             nc.scalar.copy(rows[t][:, :S], banks[t][:])
 
         pa = keep.tile([P, PACK, W], F32, name="pa")
         pb = keep.tile([P, PACK, W], F32, name="pb")
         rb = keep.tile([P, PACK, W], F32, name="rb")
         inv = keep.tile([P, PACK, W], F32, name="inv")
-        exps = [keep.tile([P, 3, S], F32, name=f"exps{t}") for t in tiles]
+        size = keep.tile([P, PACK, W], F32, name="size")
+        root = keep.tile([P, PACK, W], F32, name="root")
+        exps = [keep.tile([P, 2, S], F32, name=f"exps{t}") for t in tiles]
+        ex4 = [keep.tile([P, S], F32, name=f"ex4_{t}") for t in tiles]
         for t in tiles:
             nc.vector.tensor_copy(pb[:, t, :], rows[t][:].indirect(n2_sb[:]))
         for t in tiles:
             nc.vector.tensor_copy(pa[:, t, :], rows[t][:].indirect(n1_sb[:]))
-        for t in tiles:
-            size = exps[t][:, 0:2, 0 : W // 2]
-            root = exps[t][:, 2, 0:W]
-            nc.scalar.activation(size, pb[:, t, :].rearrange("p (a b) -> p a b", a=2), ACT.Abs)
-            nc.scalar.activation(root.rearrange("p (a b) -> p a b", a=2), size, ACT.Abs_reciprocal_sqrt, bias=0.5)
-            nc.scalar.activation(inv[:, t, :], root, ACT.Square)
         for u in range(2):
             pair = slice(2 * u, 2 * u + 2)
             nc.vector.tensor_tensor(rb[:, pair, :], pa[:, pair, :], pb[:, pair, :], ALU.max)
         dt = [keep.tile([P, S], F32, name=f"dt{t}") for t in tiles]
         for t in tiles:
-            nc.vector.tensor_tensor(dt[t][:].indirect(n1_sb[:]), pa[:, t, :], inv[:, t, :], ALU.mult)
-        for t in tiles:
             nc.vector.tensor_copy(dt[t][:].indirect(n2_sb[:]), rb[:, t, :])
 
         for t in tiles:
-            nc.scalar.activation(exps[t][:, 0, :], banks[t][:], ACT.Exp, scale=0.5)
+            nc.scalar.activation(exps[t][:, 0, :], rows[t][:, :S], ACT.Exp, scale=0.5)
             nc.scalar.activation(exps[t][:, 1, :], rows[t][:].indirect(n3_sb[:]), ACT.Exp, scale=0.5)
-            nc.scalar.activation(exps[t][:, 2, :], rows[t][:].indirect(n4_sb[:]), ACT.Exp, scale=0.5)
+            if t < SCALAR_N4:
+                nc.scalar.activation(ex4[t][:], rows[t][:].indirect(n4_sb[:]), ACT.Exp, scale=0.5)
+            else:
+                nc.vector.tensor_copy(ex4[t][:], exps[t][:].rearrange("p e c -> p (e c)").indirect(n4_sb[:]))
             for b in range(4):
                 cols = slice(P * b, P * (b + 1))
-                for e in range(3):
+                terms = (exps[t][:, 0, cols], exps[t][:, 1, cols], ex4[t][:, cols])
+                for e, term in enumerate(terms):
                     nc.tensor.matmul(
-                        banks[4 + b][:, P * t : P * (t + 1)], lhsT=exps[t][:, e, cols], rhs=ident[:],
+                        banks[4 + b][:, P * t : P * (t + 1)], lhsT=term, rhs=ident[:],
                         start=(e == 0), stop=(e == 2), is_transpose=True,
                     )
 
-        zz = keep.tile([P, PACK, S], BF16, name="zz")
-        for t in range(LAST):
-            nc.gpsimd.tensor_scalar(zz[:, t, :], dt[t][:], ga_sb[:, t : t + 1], 0.0, ALU.mult, ALU.add)
-        nc.vector.tensor_scalar(zz[:, LAST, :], dt[LAST][:], ga_sb[:, LAST : LAST + 1], None, ALU.mult)
-        zi = keep.tile([P, S, PACK], BF16, name="zi", align_bytes=64)
-        nc.vector.tensor_copy(
-            zi[:].rearrange("p (u m) t -> p m u t", u=PACK), zz[:].rearrange("p t (m u) -> p m u t", u=PACK)
-        )
-        zq = keep.tile([P, S], U32, name="zq", align_bytes=64)
-        zs = keep.tile([P, S], U8, name="zs", align_bytes=64)
-        nc.vector.quantize_mx(zq[:].bitcast(FP8X4), zs[:], zi[:].rearrange("p c t -> p (c t)"))
+        for t in tiles:
+            nc.scalar.activation(size[:, t, :], pb[:, t, :], ACT.Abs)
+            nc.scalar.activation(root[:, t, :], size[:, t, :], ACT.Abs_reciprocal_sqrt, bias=0.5)
+            nc.scalar.activation(inv[:, t, :], root[:, t, :], ACT.Square)
+            nc.vector.tensor_tensor(dt[t][:].indirect(n1_sb[:]), pa[:, t, :], inv[:, t, :], ALU.mult)
 
-        turned = [keep.tile([P, H], F32, name=f"turned{b}") for b in range(4)]
+        turned = keep.tile([P, 4, H], F32, name="turned")
         share = keep.tile([P, PACK, S], F32, name="share")
         for step in range(5):
             if step < 4:
                 b = step
-                nc.scalar.activation(turned[b][:], banks[4 + b][:], ACT.Abs_reciprocal_sqrt, scale=0.5)
+                nc.scalar.activation(turned[:, b, :], banks[4 + b][:], ACT.Abs_reciprocal_sqrt, scale=0.5)
                 for t in tiles:
                     feats = slice(P * t, P * (t + 1))
-                    nc.tensor.transpose(banks[b][:, feats], turned[b][:, feats], ident[:])
+                    nc.tensor.transpose(banks[b][:, feats], turned[:, b, feats], ident[:])
             if step >= 1:
                 b = step - 1
                 nc.scalar.activation(
                     share[:, :, P * b : P * (b + 1)], banks[b][:].rearrange("p (t c) -> p t c", t=PACK), ACT.Square
                 )
 
+        zz = turned[:, 2:, :].rearrange("p b c -> p (b c)").bitcast(BF16).rearrange("p (t c) -> p t c", t=PACK)
+        for t in range(LAST):
+            nc.scalar.activation(zz[:, t, :], dt[t][:], ACT.Copy, scale=ga_sb[:, t : t + 1])
+        for t in range(LAST, PACK):
+            nc.vector.tensor_scalar(zz[:, t, :], dt[t][:], ga_sb[:, t : t + 1], None, ALU.mult)
+
         z2z = keep.tile([P, PACK, S], BF16, name="z2z")
-        z2i = keep.tile([P, S, PACK], BF16, name="z2i", align_bytes=64)
+        z2i = [keep.tile([P, HALF, PACK], BF16, name=f"z2i{h}", align_bytes=64) for h in range(2)]
         z2q = keep.tile([P, S], U32, name="z2q", align_bytes=64)
         z2s = keep.tile([P, S], U8, name="z2s", align_bytes=64)
-        for b in range(4):
-            places = slice(P * b, P * (b + 1))
+        for h in range(2):
+            half = slice(HALF * h, HALF * (h + 1))
             for t in tiles:
                 nc.vector.scalar_tensor_tensor(
-                    z2z[:, t, places], share[:, t, places], gb_sb[:, t : t + 1], exps[t][:, 0, places], ALU.mult, ALU.mult
+                    z2z[:, t, half], share[:, t, half], gb_sb[:, t : t + 1], exps[t][:, 0, half], ALU.mult, ALU.mult
                 )
-            nc.vector.tensor_copy(z2i[:, places, :], z2z[:, :, places].rearrange("p t c -> p c t"))
-            nc.vector.quantize_mx(
-                z2q[:, places].bitcast(FP8X4), z2s[:, places], z2i[:, places, :].rearrange("p c t -> p (c t)")
-            )
-            if b == LAST:
-                for u in tiles:
-                    nc.scalar.activation(rows[u][:, : P * LAST], banks[4 + u][:, : P * LAST], ACT.Copy, scale=0.0625)
-            for u in tiles:
-                cols = slice(P * u, P * (u + 1))
-                nc.tensor.matmul_mx(
-                    banks[4 + u][:, places], lhsT=zq[:, cols].bitcast(FP8X4), lhsT_scale=zs[:, cols],
-                    rhs=z2q[:, places].bitcast(FP8X4), rhs_scale=z2s[:, places], start=True, stop=True,
-                )
-        for u in tiles:
-            nc.scalar.activation(rows[u][:, P * LAST : S], banks[4 + u][:, P * LAST :], ACT.Copy, scale=0.0625)
+        for b in range(4):
+            copy = nc.vector.tensor_copy if b == 2 else nc.scalar.copy
+            copy(z2i[b // 2][:, P * (b % 2) : P * (b % 2 + 1), :], z2z[:, :, P * b : P * (b + 1)].rearrange("p t c -> p c t"))
 
-        second = [keep.tile([P, S], F32, name=f"second{u}") for u in tiles]
-        diff = [keep.tile([P, S], F32, name=f"diff{u}") for u in tiles]
-        result = [keep.tile([P, S], F32, name=f"result{u}") for u in tiles]
+        zq = keep.tile([P, S], U32, name="zq", align_bytes=64)
+        zs = keep.tile([P, S], U8, name="zs", align_bytes=64)
+        zz_view = zz.rearrange("p t (m u) -> p u m t", u=PACK)
+
+        def quantize_z(first, count, grouped, copy):
+            cols = slice(P * first, P * (first + count))
+            copy(grouped.rearrange("p (u m t) -> p m u t", u=count, t=PACK), zz_view[:, first : first + count].rearrange("p u m t -> p m u t"))
+            nc.vector.quantize_mx(zq[:, cols].bitcast(FP8X4), zs[:, cols], grouped)
+
+        signed = {u: keep.tile([P, 2, S], F32, name=f"signed{u}") for u in SUMMED}
+
+        def product(u, places, bank):
+            cols = slice(P * u, P * (u + 1))
+            nc.tensor.matmul_mx(
+                bank[:, places], lhsT=zq[:, cols].bitcast(FP8X4), lhsT_scale=zs[:, cols],
+                rhs=z2q[:, places].bitcast(FP8X4), rhs_scale=z2s[:, places], start=True, stop=True,
+            )
+            nc.scalar.activation(rows[u][:, places], bank[:, places], ACT.Copy, scale=0.0625)
+            if u in SUMMED:
+                nc.scalar.activation(signed[u][:, 0, places], bank[:, places], ACT.Copy, scale=0.0625)
+                nc.scalar.activation(signed[u][:, 1, places], bank[:, places], ACT.Copy, scale=-0.0625)
+
+        zi_first = keep.tile([P, H], BF16, name="zi_first", align_bytes=64)
+        quantize_z(0, 1, zi_first[:], nc.vector.tensor_copy)
+        late = z2i[1][:].rearrange("p c t -> p (c t)")
+        pieces = (
+            (slice(0, HALF), z2i[0][:].rearrange("p c t -> p (c t)"), banks[4]),
+            (slice(HALF, HALF + P), late[:, :H], banks[1]),
+            (slice(HALF + P, S), late[:, H:], banks[0]),
+        )
+        for places, grouped, bank in pieces:
+            nc.vector.quantize_mx(z2q[:, places].bitcast(FP8X4), z2s[:, places], grouped)
+            product(0, places, bank)
+        for u in (1, 2):
+            quantize_z(u, 1, late[:, H * (u - 1) : H * u], nc.vector.tensor_copy)
+            product(u, slice(0, S), banks[4 + u])
+        zi_last = keep.tile([P, H], BF16, name="zi_last", align_bytes=64)
+        quantize_z(LAST, 1, zi_last[:], nc.scalar.copy)
+        product(LAST, slice(0, S), banks[4 + LAST])
+
         out_rows = out.rearrange("(p u) c -> u p c", u=PACK)
-        for step in range(PACK + 2):
-            if step < PACK:
-                nc.vector.tensor_copy(second[step][:], rows[step][:].indirect(n6_sb[:]))
-            if 1 <= step <= PACK:
-                u = step - 1
-                nc.vector.tensor_tensor(diff[u][:], rows[u][:].indirect(n5_sb[:]), second[u][:], ALU.subtract)
-            if step >= 2:
-                u = step - 2
-                engine = nc.gpsimd if u < 2 else nc.vector
-                engine.tensor_tensor(result[u][:], diff[u][:], rows[u][:, :S], ALU.mult)
-                nc.sync.dma_start(out_rows[u], result[u][:])
+        result = [keep.tile([P, S], F32, name=f"result{u}") for u in tiles]
+
+        second = {u: keep.tile([P, S], F32, name=f"second{u}") for u in (0, LAST)}
+
+        def finish_on_vector(u, diff, pieces):
+            width = S // pieces
+            spans = [slice(width * i, width * (i + 1)) for i in range(pieces)]
+            for span in spans:
+                entries = n5_sb[:, span.start // 16 : span.stop // 16]
+                nc.vector.tensor_tensor(diff[:, span], rows[u][:].indirect(entries), second[u][:, span], ALU.subtract)
+            for span in spans:
+                nc.vector.tensor_tensor(result[u][:, span], diff[:, span], rows[u][:, span], ALU.mult)
+                nc.sync.dma_start(out_rows[u][:, span], result[u][:, span])
+
+        def finish_on_tensor(u):
+            terms = keep.tile([P, 2, S], F32, name=f"terms{u}")
+            for e, entries in enumerate((n5_sb, n6_sb)):
+                nc.vector.tensor_tensor(terms[:, e, :], rows[u][:].indirect(entries[:]), signed[u][:, e, :], ALU.mult)
+                for b in range(4):
+                    nc.tensor.matmul(
+                        banks[b][:, :P], lhsT=terms[:, e, P * b : P * (b + 1)], rhs=ident[:],
+                        start=(e == 0), stop=(e == 1), is_transpose=True,
+                    )
+            flipped = keep.tile([P, S], F32, name=f"flipped{u}")
+            for b in range(4):
+                cols = slice(P * b, P * (b + 1))
+                nc.scalar.copy(flipped[:, cols], banks[b][:, :P])
+                nc.tensor.transpose(banks[4 + u][:, cols], flipped[:, cols], ident[:])
+            nc.scalar.copy(result[u][:], banks[4 + u][:])
+            nc.sync.dma_start(out_rows[u], result[u][:])
+
+        nc.vector.tensor_copy(second[0][:], rows[0][:].indirect(n6_sb[:]))
+        for u in SUMMED:
+            finish_on_tensor(u)
+        finish_on_vector(0, signed[2][:, 1, :], 1)
+        nc.vector.tensor_copy(second[LAST][:], rows[LAST][:].indirect(n6_sb[:]))
+        finish_on_vector(LAST, signed[1][:, 0, :], 2)

@@ -16,10 +16,14 @@ ACT = mybir.ActivationFunctionType
 
 P = 128
 PACK = 4
+LAST = PACK - 1
+QUADRANTS = 4
+CHUNKS = S // P
 HALF = S // 2
+PER_COLUMN = 16
+S_SCALE = 0.0625
 SCALAR_N4 = 3
 SUMMED = (1, 2)
-LAST = PACK - 1
 
 
 def tile_picked_selfratiosharewind_none_p_kernel(
@@ -41,8 +45,8 @@ def tile_picked_selfratiosharewind_none_p_kernel(
 
         offs_sb = load_list("offs_sb", offs)
         xs_in = keep.tile([P, T], U8, name="xs_in")
-        for q in range(4):
-            queue = nc.sync if q < 2 else nc.scalar
+        for q in range(QUADRANTS):
+            queue = nc.sync if q < QUADRANTS // 2 else nc.scalar
             queue.dma_start(xs_in[32 * q : 32 * q + 4, :].bitcast(I32), x_scales[0, 4 * q : 4 * q + 4, :].bitcast(I32))
         w_raw = keep.tile([P, PACK, H], F32, name="w_raw")
         nc.sync.dma_start(w_raw[:], w1.rearrange("(p j) c -> p j c", j=PACK))
@@ -63,33 +67,33 @@ def tile_picked_selfratiosharewind_none_p_kernel(
         nc.sync.dma_start(gb_sb[:], gb.rearrange("(p t) o -> p (t o)", t=PACK))
 
         rows = [keep.tile([P, 2 * S], F32, name=f"rows{t}") for t in tiles]
-        for t in tiles:
-            nc.gpsimd.memset(rows[t][:, S:], 0.0)
-
         xs = keep.tile([P, T], U8, name="xs")
         nc.vector.memset(xs[:].bitcast(I32), 0)
-        for q in range(4):
+        for t in tiles:
+            engine = nc.vector if t < PACK // 2 else nc.gpsimd
+            engine.memset(rows[t][:, S:], 0.0)
+        for q in range(QUADRANTS):
             nc.vector.tensor_copy(xs[32 * q : 32 * q + 4, :].bitcast(I32), xs_in[32 * q : 32 * q + 4, :].bitcast(I32))
         xsg = keep.tile([P, S], U8, name="xsg", align_bytes=64)
         nc.vector.tensor_copy(xsg[:], xs[:].indirect(offs_sb[:]))
+
         wq = keep.tile([P, H], U32, name="wq", align_bytes=64)
         ws = keep.tile([P, H], U8, name="ws", align_bytes=64)
         w_view = w_raw[:].rearrange("p j (m t) -> p m t j", t=PACK)
         for g, copy in enumerate((nc.vector.tensor_copy, nc.scalar.copy)):
             wi = keep.tile([P, 2, P, PACK], BF16, name=f"wi{g}", align_bytes=64)
             copy(wi[:].rearrange("p t m j -> p m t j"), w_view[:, :, 2 * g : 2 * g + 2, :])
-            cols = slice(2 * P * g, 2 * P * (g + 1))
-            nc.vector.quantize_mx(wq[:, cols].bitcast(FP8X4), ws[:, cols], wi[:].rearrange("p t m j -> p (t m j)"))
+            feats = slice(2 * P * g, 2 * P * (g + 1))
+            nc.vector.quantize_mx(wq[:, feats].bitcast(FP8X4), ws[:, feats], wi[:].rearrange("p t m j -> p (t m j)"))
         xg = keep.tile([P, S], U32, name="xg", align_bytes=64)
         for h in range(2):
-            entries = offs_sb[:, HALF // 16 * h : HALF // 16 * (h + 1)]
+            entries = offs_sb[:, HALF // PER_COLUMN * h : HALF // PER_COLUMN * (h + 1)]
             nc.vector.tensor_copy(xg[:, HALF * h : HALF * (h + 1)], xw[:].bitcast(U32).indirect(entries))
 
-
         def project(t, places, bank):
-            cols = slice(P * t, P * (t + 1))
+            feats = slice(P * t, P * (t + 1))
             nc.tensor.matmul_mx(
-                bank[:, places], lhsT=wq[:, cols].bitcast(FP8X4), lhsT_scale=ws[:, cols],
+                bank[:, places], lhsT=wq[:, feats].bitcast(FP8X4), lhsT_scale=ws[:, feats],
                 rhs=xg[:, places].bitcast(FP8X4), rhs_scale=xsg[:, places], start=True, stop=True,
             )
 
@@ -99,9 +103,9 @@ def tile_picked_selfratiosharewind_none_p_kernel(
         nc.vector.tensor_copy(rows[0][:, HALF:S], banks[0][:, HALF:])
         for t in range(1, PACK):
             project(t, slice(0, S), banks[t])
-        nc.vector.tensor_copy(rows[1][:, :S], banks[1][:])
-        for t in range(2, PACK):
-            nc.scalar.copy(rows[t][:, :S], banks[t][:])
+        for t in range(1, LAST):
+            nc.vector.tensor_copy(rows[t][:, :S], banks[t][:])
+        nc.scalar.copy(rows[LAST][:, :S], banks[LAST][:])
 
         pa = keep.tile([P, PACK, W], F32, name="pa")
         pb = keep.tile([P, PACK, W], F32, name="pb")
@@ -109,19 +113,19 @@ def tile_picked_selfratiosharewind_none_p_kernel(
         inv = keep.tile([P, PACK, W], F32, name="inv")
         size = keep.tile([P, PACK, W], F32, name="size")
         root = keep.tile([P, PACK, W], F32, name="root")
-        exps = [keep.tile([P, 2, S], F32, name=f"exps{t}") for t in tiles]
-        ex4 = [keep.tile([P, S], F32, name=f"ex4_{t}") for t in tiles]
         for t in tiles:
             nc.vector.tensor_copy(pb[:, t, :], rows[t][:].indirect(n2_sb[:]))
         for t in tiles:
             nc.vector.tensor_copy(pa[:, t, :], rows[t][:].indirect(n1_sb[:]))
-        for u in range(2):
-            pair = slice(2 * u, 2 * u + 2)
+        for g in range(2):
+            pair = slice(2 * g, 2 * g + 2)
             nc.vector.tensor_tensor(rb[:, pair, :], pa[:, pair, :], pb[:, pair, :], ALU.max)
         dt = [keep.tile([P, S], F32, name=f"dt{t}") for t in tiles]
         for t in tiles:
             nc.vector.tensor_copy(dt[t][:].indirect(n2_sb[:]), rb[:, t, :])
 
+        exps = [keep.tile([P, 2, S], F32, name=f"exps{t}") for t in tiles]
+        ex4 = [keep.tile([P, S], F32, name=f"ex4_{t}") for t in tiles]
         for t in tiles:
             nc.scalar.activation(exps[t][:, 0, :], rows[t][:, :S], ACT.Exp, scale=0.5)
             nc.scalar.activation(exps[t][:, 1, :], rows[t][:].indirect(n3_sb[:]), ACT.Exp, scale=0.5)
@@ -129,12 +133,10 @@ def tile_picked_selfratiosharewind_none_p_kernel(
                 nc.scalar.activation(ex4[t][:], rows[t][:].indirect(n4_sb[:]), ACT.Exp, scale=0.5)
             else:
                 nc.vector.tensor_copy(ex4[t][:], exps[t][:].rearrange("p e c -> p (e c)").indirect(n4_sb[:]))
-            for b in range(4):
-                cols = slice(P * b, P * (b + 1))
-                terms = (exps[t][:, 0, cols], exps[t][:, 1, cols], ex4[t][:, cols])
-                for e, term in enumerate(terms):
+            for e, term in enumerate((exps[t][:, 0, :], exps[t][:, 1, :], ex4[t][:])):
+                for b in range(CHUNKS):
                     nc.tensor.matmul(
-                        banks[4 + b][:, P * t : P * (t + 1)], lhsT=term, rhs=ident[:],
+                        banks[4 + b][:, P * t : P * (t + 1)], lhsT=term[:, P * b : P * (b + 1)], rhs=ident[:],
                         start=(e == 0), stop=(e == 2), is_transpose=True,
                     )
 
@@ -144,26 +146,32 @@ def tile_picked_selfratiosharewind_none_p_kernel(
             nc.scalar.activation(inv[:, t, :], root[:, t, :], ACT.Square)
             nc.vector.tensor_tensor(dt[t][:].indirect(n1_sb[:]), pa[:, t, :], inv[:, t, :], ALU.mult)
 
-        turned = keep.tile([P, 4, H], F32, name="turned")
+        turned = keep.tile([P, CHUNKS, H], F32, name="turned")
         share = keep.tile([P, PACK, S], F32, name="share")
-        for step in range(5):
-            if step < 4:
-                b = step
-                nc.scalar.activation(turned[:, b, :], banks[4 + b][:], ACT.Abs_reciprocal_sqrt, scale=0.5)
-                for t in tiles:
-                    feats = slice(P * t, P * (t + 1))
-                    nc.tensor.transpose(banks[b][:, feats], turned[:, b, feats], ident[:])
-            if step >= 1:
-                b = step - 1
-                nc.scalar.activation(
-                    share[:, :, P * b : P * (b + 1)], banks[b][:].rearrange("p (t c) -> p t c", t=PACK), ACT.Square
-                )
+
+        def take_root(b):
+            nc.scalar.activation(turned[:, b, :], banks[4 + b][:], ACT.Abs_reciprocal_sqrt, scale=0.5)
+            for t in tiles:
+                feats = slice(P * t, P * (t + 1))
+                nc.tensor.transpose(banks[b][:, feats], turned[:, b, feats], ident[:])
+
+        def square(b):
+            nc.scalar.activation(
+                share[:, :, P * b : P * (b + 1)], banks[b][:].rearrange("p (t c) -> p t c", t=PACK), ACT.Square
+            )
+
+        for b in range(CHUNKS - 1):
+            take_root(b)
+        for b in range(CHUNKS // 2):
+            square(b)
+        take_root(CHUNKS - 1)
+        for b in range(CHUNKS // 2, CHUNKS):
+            square(b)
 
         zz = turned[:, 2:, :].rearrange("p b c -> p (b c)").bitcast(BF16).rearrange("p (t c) -> p t c", t=PACK)
         for t in range(LAST):
             nc.scalar.activation(zz[:, t, :], dt[t][:], ACT.Copy, scale=ga_sb[:, t : t + 1])
-        for t in range(LAST, PACK):
-            nc.vector.tensor_scalar(zz[:, t, :], dt[t][:], ga_sb[:, t : t + 1], None, ALU.mult)
+        nc.vector.tensor_scalar(zz[:, LAST, :], dt[LAST][:], ga_sb[:, LAST : LAST + 1], None, ALU.mult)
 
         z2z = keep.tile([P, PACK, S], BF16, name="z2z")
         z2i = [keep.tile([P, HALF, PACK], BF16, name=f"z2i{h}", align_bytes=64) for h in range(2)]
@@ -175,34 +183,34 @@ def tile_picked_selfratiosharewind_none_p_kernel(
                 nc.vector.scalar_tensor_tensor(
                     z2z[:, t, half], share[:, t, half], gb_sb[:, t : t + 1], exps[t][:, 0, half], ALU.mult, ALU.mult
                 )
-        for b in range(4):
-            copy = nc.vector.tensor_copy if b == 2 else nc.scalar.copy
+        for b in range(CHUNKS):
+            copy = nc.vector.tensor_copy if b == CHUNKS // 2 else nc.scalar.copy
             copy(z2i[b // 2][:, P * (b % 2) : P * (b % 2 + 1), :], z2z[:, :, P * b : P * (b + 1)].rearrange("p t c -> p c t"))
 
         zq = keep.tile([P, S], U32, name="zq", align_bytes=64)
         zs = keep.tile([P, S], U8, name="zs", align_bytes=64)
         zz_view = zz.rearrange("p t (m u) -> p u m t", u=PACK)
 
-        def quantize_z(first, count, grouped, copy):
-            cols = slice(P * first, P * (first + count))
-            copy(grouped.rearrange("p (u m t) -> p m u t", u=count, t=PACK), zz_view[:, first : first + count].rearrange("p u m t -> p m u t"))
-            nc.vector.quantize_mx(zq[:, cols].bitcast(FP8X4), zs[:, cols], grouped)
+        def quantize_z(u, grouped, copy):
+            s_rows = slice(P * u, P * (u + 1))
+            copy(grouped.rearrange("p (m t) -> p m t", t=PACK), zz_view[:, u])
+            nc.vector.quantize_mx(zq[:, s_rows].bitcast(FP8X4), zs[:, s_rows], grouped)
 
         signed = {u: keep.tile([P, 2, S], F32, name=f"signed{u}") for u in SUMMED}
 
         def product(u, places, bank):
-            cols = slice(P * u, P * (u + 1))
+            s_rows = slice(P * u, P * (u + 1))
             nc.tensor.matmul_mx(
-                bank[:, places], lhsT=zq[:, cols].bitcast(FP8X4), lhsT_scale=zs[:, cols],
+                bank[:, places], lhsT=zq[:, s_rows].bitcast(FP8X4), lhsT_scale=zs[:, s_rows],
                 rhs=z2q[:, places].bitcast(FP8X4), rhs_scale=z2s[:, places], start=True, stop=True,
             )
-            nc.scalar.activation(rows[u][:, places], bank[:, places], ACT.Copy, scale=0.0625)
+            nc.scalar.activation(rows[u][:, places], bank[:, places], ACT.Copy, scale=S_SCALE)
             if u in SUMMED:
-                nc.scalar.activation(signed[u][:, 0, places], bank[:, places], ACT.Copy, scale=0.0625)
-                nc.scalar.activation(signed[u][:, 1, places], bank[:, places], ACT.Copy, scale=-0.0625)
+                nc.scalar.activation(signed[u][:, 0, places], bank[:, places], ACT.Copy, scale=S_SCALE)
+                nc.scalar.activation(signed[u][:, 1, places], bank[:, places], ACT.Copy, scale=-S_SCALE)
 
         zi_first = keep.tile([P, H], BF16, name="zi_first", align_bytes=64)
-        quantize_z(0, 1, zi_first[:], nc.vector.tensor_copy)
+        quantize_z(0, zi_first[:], nc.vector.tensor_copy)
         late = z2i[1][:].rearrange("p c t -> p (c t)")
         pieces = (
             (slice(0, HALF), z2i[0][:].rearrange("p c t -> p (c t)"), banks[4]),
@@ -212,23 +220,22 @@ def tile_picked_selfratiosharewind_none_p_kernel(
         for places, grouped, bank in pieces:
             nc.vector.quantize_mx(z2q[:, places].bitcast(FP8X4), z2s[:, places], grouped)
             product(0, places, bank)
-        for u in (1, 2):
-            quantize_z(u, 1, late[:, H * (u - 1) : H * u], nc.vector.tensor_copy)
+        for u in SUMMED:
+            quantize_z(u, late[:, H * (u - 1) : H * u], nc.vector.tensor_copy)
             product(u, slice(0, S), banks[4 + u])
         zi_last = keep.tile([P, H], BF16, name="zi_last", align_bytes=64)
-        quantize_z(LAST, 1, zi_last[:], nc.scalar.copy)
+        quantize_z(LAST, zi_last[:], nc.scalar.copy)
         product(LAST, slice(0, S), banks[4 + LAST])
 
         out_rows = out.rearrange("(p u) c -> u p c", u=PACK)
         result = [keep.tile([P, S], F32, name=f"result{u}") for u in tiles]
-
         second = {u: keep.tile([P, S], F32, name=f"second{u}") for u in (0, LAST)}
 
-        def finish_on_vector(u, diff, pieces):
-            width = S // pieces
-            spans = [slice(width * i, width * (i + 1)) for i in range(pieces)]
+        def finish_on_vector(u, diff, parts):
+            width = S // parts
+            spans = [slice(width * i, width * (i + 1)) for i in range(parts)]
             for span in spans:
-                entries = n5_sb[:, span.start // 16 : span.stop // 16]
+                entries = n5_sb[:, span.start // PER_COLUMN : span.stop // PER_COLUMN]
                 nc.vector.tensor_tensor(diff[:, span], rows[u][:].indirect(entries), second[u][:, span], ALU.subtract)
             for span in spans:
                 nc.vector.tensor_tensor(result[u][:, span], diff[:, span], rows[u][:, span], ALU.mult)
@@ -236,24 +243,24 @@ def tile_picked_selfratiosharewind_none_p_kernel(
 
         def finish_on_tensor(u):
             terms = keep.tile([P, 2, S], F32, name=f"terms{u}")
-            for e, entries in enumerate((n5_sb, n6_sb)):
-                nc.vector.tensor_tensor(terms[:, e, :], rows[u][:].indirect(entries[:]), signed[u][:, e, :], ALU.mult)
-                for b in range(4):
+            for e, order in enumerate((n5_sb, n6_sb)):
+                nc.vector.tensor_tensor(terms[:, e, :], rows[u][:].indirect(order[:]), signed[u][:, e, :], ALU.mult)
+                for b in range(CHUNKS):
                     nc.tensor.matmul(
                         banks[b][:, :P], lhsT=terms[:, e, P * b : P * (b + 1)], rhs=ident[:],
                         start=(e == 0), stop=(e == 1), is_transpose=True,
                     )
             flipped = keep.tile([P, S], F32, name=f"flipped{u}")
-            for b in range(4):
-                cols = slice(P * b, P * (b + 1))
-                nc.scalar.copy(flipped[:, cols], banks[b][:, :P])
-                nc.tensor.transpose(banks[4 + u][:, cols], flipped[:, cols], ident[:])
+            for b in range(CHUNKS):
+                chunk = slice(P * b, P * (b + 1))
+                nc.scalar.copy(flipped[:, chunk], banks[b][:, :P])
+                nc.tensor.transpose(banks[4 + u][:, chunk], flipped[:, chunk], ident[:])
             nc.scalar.copy(result[u][:], banks[4 + u][:])
             nc.sync.dma_start(out_rows[u], result[u][:])
 
         nc.vector.tensor_copy(second[0][:], rows[0][:].indirect(n6_sb[:]))
         for u in SUMMED:
             finish_on_tensor(u)
-        finish_on_vector(0, signed[2][:, 1, :], 1)
+        finish_on_vector(0, signed[SUMMED[1]][:, 1, :], 1)
         nc.vector.tensor_copy(second[LAST][:], rows[LAST][:].indirect(n6_sb[:]))
-        finish_on_vector(LAST, signed[1][:, 0, :], 2)
+        finish_on_vector(LAST, signed[SUMMED[0]][:, 0, :], 2)

import concourse.mybir as mybir
from concourse.masks import make_identity

K, T, S, H, W = 512, 2048, 512, 512, 256
FLOPS = 2 * K * H * S + 2 * H * S * S

F32 = mybir.dt.float32
BF16 = mybir.dt.bfloat16
I32 = mybir.dt.int32
U32 = mybir.dt.uint32
U16 = mybir.dt.uint16
U8 = mybir.dt.uint8
FP8X4 = mybir.dt.float8_e4m3fn_x4
ALU = mybir.AluOpType
ACT = mybir.ActivationFunctionType

P = 128
PACK = 4
LAST = PACK - 1
QUADRANTS = 4
CHUNKS = S // P
HALF = S // 2
PER_COLUMN = 16
S_SCALE = 0.0625
SCALAR_N4 = 3
SUMMED = (1, 2)


def tile_picked_selfratiosharewind_none_p_kernel(
    tc, x_words, x_scales, w1, ga, gb, offs, n1, n2, n3, n4, n5, n6, out
):
    nc = tc.nc
    tiles = range(PACK)
    with (
        tc.tile_pool(name="lists", bufs=1) as lists,
        tc.tile_pool(name="keep", bufs=1) as keep,
        tc.psum_pool(name="psum", bufs=1) as psum,
    ):
        banks = [psum.tile([P, S], F32, name=f"bank{b}") for b in range(8)]

        def load_list(name, src):
            tile = lists.tile(list(src.shape), U16, name=name)
            nc.sync.dma_start(tile[:], src)
            return tile

        offs_sb = load_list("offs_sb", offs)
        xs_in = keep.tile([P, T], U8, name="xs_in")
        for q in range(QUADRANTS):
            queue = nc.sync if q < QUADRANTS // 2 else nc.scalar
            queue.dma_start(xs_in[32 * q : 32 * q + 4, :].bitcast(I32), x_scales[0, 4 * q : 4 * q + 4, :].bitcast(I32))
        w_raw = keep.tile([P, PACK, H], F32, name="w_raw")
        nc.sync.dma_start(w_raw[:], w1.rearrange("(p j) c -> p j c", j=PACK))
        xw = keep.tile([P, T], I32, name="xw")
        nc.sync.dma_start(xw[:], x_words[0].rearrange("p n t -> p (n t)").bitcast(I32))
        n2_sb = load_list("n2_sb", n2)
        n1_sb = load_list("n1_sb", n1)
        n3_sb = load_list("n3_sb", n3)
        n4_sb = load_list("n4_sb", n4)
        n6_sb = load_list("n6_sb", n6)
        n5_sb = load_list("n5_sb", n5)

        ident = keep.tile([P, P], F32, name="ident")
        make_identity(nc, ident[:])
        ga_sb = keep.tile([P, PACK], F32, name="ga_sb")
        gb_sb = keep.tile([P, PACK], F32, name="gb_sb")
        nc.sync.dma_start(ga_sb[:], ga.rearrange("(p t) o -> p (t o)", t=PACK))
        nc.sync.dma_start(gb_sb[:], gb.rearrange("(p t) o -> p (t o)", t=PACK))

        rows = [keep.tile([P, 2 * S], F32, name=f"rows{t}") for t in tiles]
        xs = keep.tile([P, T], U8, name="xs")
        nc.vector.memset(xs[:].bitcast(I32), 0)
        for t in tiles:
            engine = nc.vector if t < PACK // 2 else nc.gpsimd
            engine.memset(rows[t][:, S:], 0.0)
        for q in range(QUADRANTS):
            nc.vector.tensor_copy(xs[32 * q : 32 * q + 4, :].bitcast(I32), xs_in[32 * q : 32 * q + 4, :].bitcast(I32))
        xsg = keep.tile([P, S], U8, name="xsg", align_bytes=64)
        nc.vector.tensor_copy(xsg[:], xs[:].indirect(offs_sb[:]))

        wq = keep.tile([P, H], U32, name="wq", align_bytes=64)
        ws = keep.tile([P, H], U8, name="ws", align_bytes=64)
        w_view = w_raw[:].rearrange("p j (m t) -> p m t j", t=PACK)
        for g, copy in enumerate((nc.vector.tensor_copy, nc.scalar.copy)):
            wi = keep.tile([P, 2, P, PACK], BF16, name=f"wi{g}", align_bytes=64)
            copy(wi[:].rearrange("p t m j -> p m t j"), w_view[:, :, 2 * g : 2 * g + 2, :])
            feats = slice(2 * P * g, 2 * P * (g + 1))
            nc.vector.quantize_mx(wq[:, feats].bitcast(FP8X4), ws[:, feats], wi[:].rearrange("p t m j -> p (t m j)"))
        xg = keep.tile([P, S], U32, name="xg", align_bytes=64)
        for h in range(2):
            entries = offs_sb[:, HALF // PER_COLUMN * h : HALF // PER_COLUMN * (h + 1)]
            nc.vector.tensor_copy(xg[:, HALF * h : HALF * (h + 1)], xw[:].bitcast(U32).indirect(entries))

        def project(t, places, bank):
            feats = slice(P * t, P * (t + 1))
            nc.tensor.matmul_mx(
                bank[:, places], lhsT=wq[:, feats].bitcast(FP8X4), lhsT_scale=ws[:, feats],
                rhs=xg[:, places].bitcast(FP8X4), rhs_scale=xsg[:, places], start=True, stop=True,
            )

        project(0, slice(0, HALF), banks[4])
        nc.scalar.copy(rows[0][:, :HALF], banks[4][:, :HALF])
        project(0, slice(HALF, S), banks[0])
        nc.vector.tensor_copy(rows[0][:, HALF:S], banks[0][:, HALF:])
        for t in range(1, PACK):
            project(t, slice(0, S), banks[t])
        for t in range(1, LAST):
            nc.vector.tensor_copy(rows[t][:, :S], banks[t][:])
        nc.scalar.copy(rows[LAST][:, :S], banks[LAST][:])

        pa = keep.tile([P, PACK, W], F32, name="pa")
        pb = keep.tile([P, PACK, W], F32, name="pb")
        rb = keep.tile([P, PACK, W], F32, name="rb")
        inv = keep.tile([P, PACK, W], F32, name="inv")
        size = keep.tile([P, PACK, W], F32, name="size")
        root = keep.tile([P, PACK, W], F32, name="root")
        for t in tiles:
            nc.vector.tensor_copy(pb[:, t, :], rows[t][:].indirect(n2_sb[:]))
        for t in tiles:
            nc.vector.tensor_copy(pa[:, t, :], rows[t][:].indirect(n1_sb[:]))
        for g in range(2):
            pair = slice(2 * g, 2 * g + 2)
            nc.vector.tensor_tensor(rb[:, pair, :], pa[:, pair, :], pb[:, pair, :], ALU.max)
        dt = [keep.tile([P, S], F32, name=f"dt{t}") for t in tiles]
        for t in tiles:
            nc.vector.tensor_copy(dt[t][:].indirect(n2_sb[:]), rb[:, t, :])

        exps = [keep.tile([P, 2, S], F32, name=f"exps{t}") for t in tiles]
        ex4 = [keep.tile([P, S], F32, name=f"ex4_{t}") for t in tiles]
        for t in tiles:
            nc.scalar.activation(exps[t][:, 0, :], rows[t][:, :S], ACT.Exp, scale=0.5)
            nc.scalar.activation(exps[t][:, 1, :], rows[t][:].indirect(n3_sb[:]), ACT.Exp, scale=0.5)
            if t < SCALAR_N4:
                nc.scalar.activation(ex4[t][:], rows[t][:].indirect(n4_sb[:]), ACT.Exp, scale=0.5)
            else:
                nc.vector.tensor_copy(ex4[t][:], exps[t][:].rearrange("p e c -> p (e c)").indirect(n4_sb[:]))
            for e, term in enumerate((exps[t][:, 0, :], exps[t][:, 1, :], ex4[t][:])):
                for b in range(CHUNKS):
                    nc.tensor.matmul(
                        banks[4 + b][:, P * t : P * (t + 1)], lhsT=term[:, P * b : P * (b + 1)], rhs=ident[:],
                        start=(e == 0), stop=(e == 2), is_transpose=True,
                    )

        for t in tiles:
            nc.scalar.activation(size[:, t, :], pb[:, t, :], ACT.Abs)
            nc.scalar.activation(root[:, t, :], size[:, t, :], ACT.Abs_reciprocal_sqrt, bias=0.5)
            nc.scalar.activation(inv[:, t, :], root[:, t, :], ACT.Square)
            nc.vector.tensor_tensor(dt[t][:].indirect(n1_sb[:]), pa[:, t, :], inv[:, t, :], ALU.mult)

        turned = keep.tile([P, CHUNKS, H], F32, name="turned")
        share = keep.tile([P, PACK, S], F32, name="share")

        def take_root(b):
            nc.scalar.activation(turned[:, b, :], banks[4 + b][:], ACT.Abs_reciprocal_sqrt, scale=0.5)
            for t in tiles:
                feats = slice(P * t, P * (t + 1))
                nc.tensor.transpose(banks[b][:, feats], turned[:, b, feats], ident[:])

        def square(b):
            nc.scalar.activation(
                share[:, :, P * b : P * (b + 1)], banks[b][:].rearrange("p (t c) -> p t c", t=PACK), ACT.Square
            )

        for b in range(CHUNKS - 1):
            take_root(b)
        for b in range(CHUNKS // 2):
            square(b)
        take_root(CHUNKS - 1)
        for b in range(CHUNKS // 2, CHUNKS):
            square(b)

        zz = turned[:, 2:, :].rearrange("p b c -> p (b c)").bitcast(BF16).rearrange("p (t c) -> p t c", t=PACK)
        for t in range(LAST):
            nc.scalar.activation(zz[:, t, :], dt[t][:], ACT.Copy, scale=ga_sb[:, t : t + 1])
        nc.vector.tensor_scalar(zz[:, LAST, :], dt[LAST][:], ga_sb[:, LAST : LAST + 1], None, ALU.mult)

        z2z = keep.tile([P, PACK, S], BF16, name="z2z")
        z2i = [keep.tile([P, HALF, PACK], BF16, name=f"z2i{h}", align_bytes=64) for h in range(2)]
        z2q = keep.tile([P, S], U32, name="z2q", align_bytes=64)
        z2s = keep.tile([P, S], U8, name="z2s", align_bytes=64)
        for h in range(2):
            half = slice(HALF * h, HALF * (h + 1))
            for t in tiles:
                nc.vector.scalar_tensor_tensor(
                    z2z[:, t, half], share[:, t, half], gb_sb[:, t : t + 1], exps[t][:, 0, half], ALU.mult, ALU.mult
                )
        for b in range(CHUNKS):
            copy = nc.vector.tensor_copy if b == CHUNKS // 2 else nc.scalar.copy
            copy(z2i[b // 2][:, P * (b % 2) : P * (b % 2 + 1), :], z2z[:, :, P * b : P * (b + 1)].rearrange("p t c -> p c t"))

        zq = keep.tile([P, S], U32, name="zq", align_bytes=64)
        zs = keep.tile([P, S], U8, name="zs", align_bytes=64)
        zz_view = zz.rearrange("p t (m u) -> p u m t", u=PACK)

        def quantize_z(u, grouped, copy):
            s_rows = slice(P * u, P * (u + 1))
            copy(grouped.rearrange("p (m t) -> p m t", t=PACK), zz_view[:, u])
            nc.vector.quantize_mx(zq[:, s_rows].bitcast(FP8X4), zs[:, s_rows], grouped)

        signed = {u: keep.tile([P, 2, S], F32, name=f"signed{u}") for u in SUMMED}

        def product(u, places, bank):
            s_rows = slice(P * u, P * (u + 1))
            nc.tensor.matmul_mx(
                bank[:, places], lhsT=zq[:, s_rows].bitcast(FP8X4), lhsT_scale=zs[:, s_rows],
                rhs=z2q[:, places].bitcast(FP8X4), rhs_scale=z2s[:, places], start=True, stop=True,
            )
            nc.scalar.activation(rows[u][:, places], bank[:, places], ACT.Copy, scale=S_SCALE)
            if u in SUMMED:
                nc.scalar.activation(signed[u][:, 0, places], bank[:, places], ACT.Copy, scale=S_SCALE)
                nc.scalar.activation(signed[u][:, 1, places], bank[:, places], ACT.Copy, scale=-S_SCALE)

        zi_first = keep.tile([P, H], BF16, name="zi_first", align_bytes=64)
        quantize_z(0, zi_first[:], nc.vector.tensor_copy)
        late = z2i[1][:].rearrange("p c t -> p (c t)")
        pieces = (
            (slice(0, HALF), z2i[0][:].rearrange("p c t -> p (c t)"), banks[4]),
            (slice(HALF, HALF + P), late[:, :H], banks[1]),
            (slice(HALF + P, S), late[:, H:], banks[0]),
        )
        for places, grouped, bank in pieces:
            nc.vector.quantize_mx(z2q[:, places].bitcast(FP8X4), z2s[:, places], grouped)
            product(0, places, bank)
        for u in SUMMED:
            quantize_z(u, late[:, H * (u - 1) : H * u], nc.vector.tensor_copy)
            product(u, slice(0, S), banks[4 + u])
        zi_last = keep.tile([P, H], BF16, name="zi_last", align_bytes=64)
        quantize_z(LAST, zi_last[:], nc.scalar.copy)
        product(LAST, slice(0, S), banks[4 + LAST])

        out_rows = out.rearrange("(p u) c -> u p c", u=PACK)
        result = [keep.tile([P, S], F32, name=f"result{u}") for u in tiles]
        second = {u: keep.tile([P, S], F32, name=f"second{u}") for u in (0, LAST)}

        def finish_on_vector(u, diff, parts):
            width = S // parts
            spans = [slice(width * i, width * (i + 1)) for i in range(parts)]
            for span in spans:
                entries = n5_sb[:, span.start // PER_COLUMN : span.stop // PER_COLUMN]
                nc.vector.tensor_tensor(diff[:, span], rows[u][:].indirect(entries), second[u][:, span], ALU.subtract)
            for span in spans:
                nc.vector.tensor_tensor(result[u][:, span], diff[:, span], rows[u][:, span], ALU.mult)
                nc.sync.dma_start(out_rows[u][:, span], result[u][:, span])

        def finish_on_tensor(u):
            terms = keep.tile([P, 2, S], F32, name=f"terms{u}")
            for e, order in enumerate((n5_sb, n6_sb)):
                nc.vector.tensor_tensor(terms[:, e, :], rows[u][:].indirect(order[:]), signed[u][:, e, :], ALU.mult)
                for b in range(CHUNKS):
                    nc.tensor.matmul(
                        banks[b][:, :P], lhsT=terms[:, e, P * b : P * (b + 1)], rhs=ident[:],
                        start=(e == 0), stop=(e == 1), is_transpose=True,
                    )
            flipped = keep.tile([P, S], F32, name=f"flipped{u}")
            for b in range(CHUNKS):
                chunk = slice(P * b, P * (b + 1))
                nc.scalar.copy(flipped[:, chunk], banks[b][:, :P])
                nc.tensor.transpose(banks[4 + u][:, chunk], flipped[:, chunk], ident[:])
            nc.scalar.copy(result[u][:], banks[4 + u][:])
            nc.sync.dma_start(out_rows[u], result[u][:])

        nc.vector.tensor_copy(second[0][:], rows[0][:].indirect(n6_sb[:]))
        for u in SUMMED:
            finish_on_tensor(u)
        finish_on_vector(0, signed[SUMMED[1]][:, 1, :], 1)
        nc.vector.tensor_copy(second[LAST][:], rows[LAST][:].indirect(n6_sb[:]))
        finish_on_vector(LAST, signed[SUMMED[0]][:, 0, :], 2)
